import numpy as np, ml_dtypes
CORES = [113,118,241,246]
N = 4
import mx_ref
NC, KT, ROOT = 128, 3, 3
BF = ml_dtypes.bfloat16
def setup_inputs(rng):
    def f(*shape):
        return mx_ref.flush((rng.standard_normal(shape, dtype=np.float32) * np.exp2(rng.integers(-2, 3, shape[:-1] + (1,)))).astype(BF))
    return {"w": f(N, 128, KT * 512), "x": f(N, 128, N * KT * 4 * NC)}
def setup_inputs_blocks(rng):
    d = setup_inputs(rng)
    for k in ("w", "x"): d[k] = mx_ref.spread(d[k], rng, 1)
    return d
def setup_inputs_wide(rng):
    d = setup_inputs(rng)
    for k in ("w", "x"): d[k] = mx_ref.flush((d[k].astype(np.float32) * np.exp2(rng.integers(-8, 9, (N, 1, 1))).astype(np.float32)).astype(BF))
    return d
def setup_inputs_zeros(rng):
    d = setup_inputs(rng); v = d["x"].reshape(N, 128, -1, 4).copy()
    v[np.broadcast_to((rng.random((N, 1, v.shape[2], 1)) < 0.33), v.shape)] = 0
    d["x"] = v.reshape(d["x"].shape)
    return d
def reference(w, x):
    y = np.zeros((N, 128, NC), np.float32)
    for r in range(N):
        for t in range(KT):
            p = mx_ref.matmul(mx_ref.quantize(w[r][:, 512 * t:512 * t + 512]), mx_ref.quantize(x[ROOT][:, 4 * NC * (KT * r + t):4 * NC * (KT * r + t) + 4 * NC]))
            y[r] = p if t == 0 else y[r] + p
    return {"y": y}

from concourse.mybir import dt

N, KT, TW = 4, 3, 128
RW = KT * TW
RB = 4 * RW

SCRATCH = {
    "xb": ("sbuf", [128, N * RB], "bfloat16"),
    "wb": ("sbuf", [128, RB], "bfloat16"),
    "oq": ("sbuf", [128, (N - 1) * RW], "float8_e4m3fn_x4"),
    "osc": ("sbuf", [128, (N - 1) * RW], "uint8"),
    "xq": ("sbuf", [128, RW], "float8_e4m3fn_x4"),
    "xs": ("sbuf", [128, RW], "uint8"),
    "wq": ("sbuf", [128, RW], "float8_e4m3fn_x4"),
    "ws": ("sbuf", [128, RW], "uint8"),
    "acc": ("psum", [128, 512], "float32"),
    "yb": ("sbuf", [128, TW], "float32"),
}
SEMAPHORES = ["lx0", "lx1", "lx2", "lx3", "lw", "q0", "q1", "q2", "q3", "qw", "arr", "sent", "mm", "cp", "st"]


def _bits(m):
    return bin(m).count("1")


def _plan(T, topo):
    root = T.cores[T.root]

    def off(c):
        return (topo.host(c), topo.chip(c)) != (topo.host(root), topo.chip(root))

    others = [r for r in range(len(T.cores)) if r != T.root]
    order = [r for r in others if off(T.cores[r])] + [r for r in others if not off(T.cores[r])]
    busy = 0
    for r in order:
        if off(T.cores[r]):
            busy |= topo.mask(root, T.cores[r])
    plan = []
    for r in order:
        m = topo.mask(root, T.cores[r])
        if not off(T.cores[r]) and _bits(m & ~busy) in (1, 2, 4, 8, 16):
            m = m & ~busy
        plan.append((r, T.cores[r], m))
    return plan


def rank_program(g, core, T, topo):
    rank = T.rank_of(core)
    if rank is None:
        return
    S = T.sem
    plan = _plan(T, topo)

    if rank == T.root:
        for k, (r, _, _) in enumerate(plan):
            g.sync.dma_start(T.xb[:, RB * r:RB * (r + 1)], T.x[:, RB * r:RB * (r + 1)]).then_inc(S["lx%d" % k], 16)
        g.sync.dma_start(T.wb[:], T.w[:]).then_inc(S.lw, 16)
        g.sync.dma_start(T.xb[:, RB * rank:RB * (rank + 1)], T.x[:, RB * rank:RB * (rank + 1)]).then_inc(S.lx3, 16)
        for k, (r, _, _) in enumerate(plan):
            g.vector.wait_ge(S["lx%d" % k], 16)
            g.vector.quantize_mx(T.oq[:, RW * k:RW * (k + 1)], T.osc[:, RW * k:RW * (k + 1)],
                                 T.xb[:, RB * r:RB * (r + 1)]).then_inc(S["q%d" % k], 1)
        g.vector.wait_ge(S.lw, 16)
        g.vector.quantize_mx(T.wq[:], T.ws[:], T.wb[:]).then_inc(S.qw, 1)
        g.vector.wait_ge(S.lx3, 16)
        g.vector.quantize_mx(T.xq[:], T.xs[:], T.xb[:, RB * rank:RB * (rank + 1)]).then_inc(S.q3, 1)
        left = 0
        for k, (r, d, m) in enumerate(plan):
            rid, pid = topo.addr(d, core)
            g.wait_ge(S["q%d" % k], 1)
            g.remote_dma(out_ap=T.xq[:].bitcast(dt.uint8), in_ap=T.oq[:, RW * k:RW * (k + 1)].bitcast(dt.uint8),
                         remote_sem=S.arr, local_sem=S.sent, pid=pid, routing_id=rid, dma_engine_mask=m)
            g.remote_dma(out_ap=T.xs[:], in_ap=T.osc[:, RW * k:RW * (k + 1)],
                         remote_sem=S.arr, local_sem=S.sent, pid=pid, routing_id=rid, dma_engine_mask=m)
            left += 2 * _bits(m)
        g.tensor.wait_ge(S.qw, 1)
        g.tensor.wait_ge(S.q3, 1)
    else:
        g.sync.dma_start(T.wb[:], T.w[:]).then_inc(S.lw, 16)
        g.vector.wait_ge(S.lw, 16)
        g.vector.quantize_mx(T.wq[:], T.ws[:], T.wb[:]).then_inc(S.qw, 1)
        mine = [m for (r, _, m) in plan if r == rank][0]
        g.tensor.wait_ge(S.qw, 1)
        g.tensor.wait_ge(S.arr, 2 * _bits(mine))

    for t in range(KT):
        c = slice(TW * t, TW * (t + 1))
        g.tensor.matmul_mx(T.acc[:, 0:TW], T.wq[:, c], T.ws[:, c], T.xq[:, c], T.xs[:, c],
                           t == 0, t == KT - 1).then_inc(S.mm, 1)
    g.vector.wait_ge(S.mm, KT)
    g.vector.tensor_copy(T.yb[:], T.acc[:, 0:TW]).then_inc(S.cp, 1)
    g.sync.wait_ge(S.cp, 1)
    g.sync.dma_start(T.y[:], T.yb[:]).then_inc(S.st, 16)
    g.sync.wait_ge(S.st, 16)
    if rank == T.root:
        g.wait_ge(S.sent, left)
